import numpy as np
import ml_dtypes


def mxq(x, axis, fmt="e4m3"):
    dtype, down = {"e4m3": (ml_dtypes.float8_e4m3fn, 7), "e5m2": (ml_dtypes.float8_e5m2, 14)}[fmt]
    v = np.moveaxis(np.asarray(x, np.float32).astype(ml_dtypes.bfloat16).astype(np.float64), axis, -1)
    blocks = v.reshape(v.shape[:-1] + (-1, 32))
    amax = np.abs(blocks).max(-1, keepdims=True)
    byte = np.maximum(np.where(amax > 0, np.frexp(amax)[1] - 1 + 127, 0) - down, 1)
    scale = np.exp2(byte - 127.0)
    codes = (blocks / scale).astype(np.float32).astype(dtype).astype(np.float64)
    return np.moveaxis((codes * scale).reshape(v.shape), -1, axis)


WIDE = False


def mx_kscale(k):
    if not WIDE:
        return np.ones(k)
    levels = np.array([10, -10, 5, -5, 0])
    if k % 512:
        return np.exp2(np.random.permutation(np.resize(levels, k // 32))).repeat(32)
    a = np.empty((k // 512, 16))
    for p in range(k // 512):
        a[p, :8] = np.random.permutation(np.resize(levels, 8))
        for g in range(8):
            far = levels[np.abs(levels - a[p, g]) >= 10]
            a[p, g + 8] = far[np.random.randint(len(far))]
    return np.exp2(a.ravel()).repeat(32)


def f64(x):
    return np.asarray(x).astype(np.float64)


def striped(idx):
    return np.tile(idx.reshape(-1, 16).T, (8, 1)).astype(np.uint16)


def unstriped(offs):
    return offs[:16].T.reshape(-1).astype(np.int64)


def striped8(idx):
    return np.concatenate([x.reshape(-1, 16).T for x in idx]).astype(np.uint16)


def runs(offs, k):
    lists = np.stack([offs[16 * r : 16 * r + 16].T.reshape(-1) for r in range(8)]).astype(np.int64)
    return lists[np.arange(k) % 512 // 64]


def pack_weight(w):
    k, n = w.shape
    w = f64(np.asarray(w, np.float32).astype(ml_dtypes.bfloat16)).reshape(k // 32, 32, n)
    amax = np.abs(w).max(1)
    byte = np.clip(np.where(amax > 0, np.frexp(amax)[1] - 1 + 127 - 7, 1), 1, 254)
    scaled = (w * np.exp2(127.0 - byte)[:, None, :]).reshape(k, n).astype(np.float32)
    words = np.ascontiguousarray(scaled.reshape(k // 512, 128, 4, n).transpose(0, 1, 3, 2)).astype(ml_dtypes.float8_e4m3fn).view(np.uint8)
    return words, np.ascontiguousarray(byte.astype(np.uint8).reshape(k // 512, 16, n))


def unpack_weight(words, scales):
    g, p, n, _ = words.shape
    vals = np.ascontiguousarray(words).view(ml_dtypes.float8_e4m3fn).astype(np.float64) * np.repeat(np.exp2(scales.astype(np.float64) - 127.0), 8, axis=1)[..., None]
    return vals.transpose(0, 1, 3, 2).reshape(g * 512, n)


def relu(v):
    return np.maximum(v, 0.0)


def sigmoid(v):
    return 1.0 / (1.0 + np.exp(-np.maximum(v, -700.0)))

def planes(y):
    n, m = y.shape
    v = y.astype(np.float32).astype(ml_dtypes.bfloat16).astype(np.float64).reshape(n // 32, 32, m)
    top = np.abs(v).max(1)
    byte = np.clip(np.where(top > 0, np.frexp(top)[1] - 1 + 127 - 7, 1), 1, 254)
    codes = (v * np.exp2(127.0 - byte)[:, None, :]).reshape(n, m).astype(np.float32).astype(ml_dtypes.float8_e4m3fn).view(np.uint8)
    words = codes.reshape(n // 512, 128, 4, m).transpose(0, 1, 3, 2)
    return np.ascontiguousarray(words), np.ascontiguousarray(byte.astype(np.uint8).reshape(n // 512, 16, m))


K, T, S, V, N, H = 512, 2048, 512, 256, 512, 512


def setup_inputs():
    n = np.random.standard_normal
    s = mx_kscale(K)[:, None]
    u = mx_kscale(H)
    packed_xT = pack_weight(n((K, T)) * s)
    packed_w1 = pack_weight(n((K, H)) / np.sqrt(K) / s)
    packed_w2 = pack_weight(n((K, H)) / np.sqrt(K) / s)
    packed_w3 = pack_weight(n((H, N)) / np.sqrt(H) / u[:, None])
    return {
        "x_words": packed_xT[0],
        "x_scales": packed_xT[1],
        "w1_words": packed_w1[0],
        "w1_scales": packed_w1[1],
        "w2_words": packed_w2[0],
        "w2_scales": packed_w2[1],
        "gn": (np.random.uniform(0.5, 1.5, (H, 1)) * u[:, None]).astype(np.float32),
        "w3_words": packed_w3[0],
        "w3_scales": packed_w3[1],
        "res": (2 * n((N, V))).astype(np.float32),
        "offs": striped(np.random.permutation(T)[:S]),
        "two": striped(np.random.permutation(T)[:S]),
        "ba": striped8(np.stack([np.random.permutation(S)[:V] for _ in range(8)])),
        "bb": striped8(np.stack([np.random.permutation(S)[:V] for _ in range(8)])),
    }


def reference(x_words, x_scales, w1_words, w1_scales, w2_words, w2_scales, gn, w3_words, w3_scales, res, offs, two, ba, bb):
    xq = unpack_weight(x_words, x_scales)[:, unstriped(offs)]
    y = unpack_weight(w1_words, w1_scales).T @ xq
    x_two = unpack_weight(x_words, x_scales)[:, unstriped(two)]
    c = sigmoid(unpack_weight(w2_words, w2_scales).T @ x_two)
    hi = y + c
    lo = y - c
    sh = relu(np.minimum(hi[np.arange(H)[:, None], runs(ba, H)], hi[np.arange(H)[:, None], runs(bb, H)]) - (np.maximum(lo[np.arange(H)[:, None], runs(ba, H)], lo[np.arange(H)[:, None], runs(bb, H)])))
    un = np.maximum(hi[np.arange(H)[:, None], runs(ba, H)], hi[np.arange(H)[:, None], runs(bb, H)]) - (np.minimum(lo[np.arange(H)[:, None], runs(ba, H)], lo[np.arange(H)[:, None], runs(bb, H)]))
    z = f64(gn) * (sh / (un + 0.1))
    out_0 = f64(res) + (unpack_weight(w3_words, w3_scales).T @ mxq(z, 0, "e4m3"))
    return (out_0,) + planes(out_0)

@@ -1,0 +1,185 @@
+from contextlib import ExitStack
+
+import concourse.mybir as mybir
+
+K, T, S, V, N, H = 512, 2048, 512, 256, 512, 512
+FLOPS = 2 * K * H * S * 2 + 2 * H * N * V
+
+F32 = mybir.dt.float32
+BF16 = mybir.dt.bfloat16
+I32 = mybir.dt.int32
+U32 = mybir.dt.uint32
+U16 = mybir.dt.uint16
+U8 = mybir.dt.uint8
+FP8X4 = mybir.dt.float8_e4m3fn_x4
+ALU = mybir.AluOpType
+ACT = mybir.ActivationFunctionType
+
+P = 128
+PACK = 4
+HALF = V // 2
+DIRECT = 1
+
+
+def tile_picked_boxiou_none_po_kernel(tc, x_words, x_scales, w1_words, w1_scales, w2_words, w2_scales, gn, w3_words, w3_scales, res, offs, two, ba, bb, out_0, out_1, out_2):
+    nc = tc.nc
+    with ExitStack() as ctx:
+        keep = ctx.enter_context(tc.tile_pool(name="keep", bufs=1))
+        psum = ctx.enter_context(tc.psum_pool(name="psum", bufs=1))
+
+        def tile(name, shape, dtype):
+            return keep.tile(shape, dtype, name=name, align_bytes=64)
+
+        def load_list(name, src):
+            dst = tile(name, list(src.shape), U16)
+            nc.sync.dma_start(dst[:], src)
+            return dst
+
+        def load_words(queue, name, src):
+            dst = tile(name, [P, src.shape[2]], I32)
+            queue.dma_start(dst[:], src[0].rearrange("p n t -> p (n t)").bitcast(I32))
+            return dst
+
+        def load_scales(queue, dst, first, src):
+            for q in range(4):
+                queue.dma_start(dst[32 * q + first : 32 * q + first + 4, :].bitcast(I32), src[0, 4 * q : 4 * q + 4, :].bitcast(I32))
+
+        def deal(name, src, dtype, run):
+            dst = tile(name, [P, PACK * P], dtype)
+            nc.vector.tensor_copy(
+                dst[:].rearrange("p (t c i) -> p c t i", t=PACK, i=run),
+                src[:].rearrange("p (c i t) -> p c t i", t=PACK, i=run),
+            )
+            return dst
+
+        xs = tile("xs", [P, T], U8)
+        nc.vector.memset(xs[:].bitcast(I32), 0)
+        ws = tile("ws", [P, H], U8)
+        nc.vector.memset(ws[:].bitcast(I32), 0)
+        w3s = tile("w3s", [P, N], U8)
+        nc.vector.memset(w3s[:].bitcast(I32), 0)
+
+        two_t = load_list("two_t", two)
+        load_scales(nc.sync, xs, 0, x_scales)
+        offs_t = load_list("offs_t", offs)
+        xw = load_words(nc.sync, "xw", x_words)
+        w2w = load_words(nc.sync, "w2w", w2_words)
+        load_scales(nc.sync, ws, 0, w2_scales)
+        load_scales(nc.scalar, ws, 4, w1_scales)
+        w1w = load_words(nc.sync, "w1w", w1_words)
+        ba_t = load_list("ba_t", ba)
+        bb_t = load_list("bb_t", bb)
+        w3w = load_words(nc.sync, "w3w", w3_words)
+        load_scales(nc.sync, w3s, 0, w3_scales)
+        gain = tile("gain", [P, PACK], F32)
+        nc.sync.dma_start(gain[:], gn.rearrange("(p t) o -> p (t o)", t=PACK))
+        resid = tile("resid", [P, PACK, V], F32)
+        nc.sync.dma_start(resid[:], res.rearrange("(p t) v -> p t v", t=PACK))
+
+        def pick(name, window, dtype, lst):
+            dst = tile(name, [P, S], dtype)
+            nc.vector.tensor_copy(dst[:], window.indirect(lst[:]))
+            return dst
+
+        two_s = pick("two_s", xs[:], U8, two_t)
+        idx_s = pick("idx_s", xs[:], U8, offs_t)
+        two_w = pick("two_w", xw[:].bitcast(U32), U32, two_t)
+        w2d = deal("w2d", w2w, I32, 4)
+        wsd = deal("wsd", ws, U8, 16)
+
+        def project(t, bank, wd, first, xw_p, xs_p):
+            acc = psum.tile([P, S], F32, name="acc%d" % bank, tag="bank%d" % bank)
+            cols = slice(t * P, (t + 1) * P)
+            nc.tensor.matmul_mx(out=acc[:], lhsT=wd[:, cols].bitcast(FP8X4), lhsT_scale=wsd[first:P, cols],
+                                rhs=xw_p[:].bitcast(FP8X4), rhs_scale=xs_p[:], start=True, stop=True)
+            return acc
+
+        c_a = tile("c_a", [P, PACK, V], F32)
+        c_b = tile("c_b", [P, PACK, V], F32)
+        u_rows = []
+        for t in range(PACK):
+            acc = project(t, t, w2d, 0, two_w, two_s)
+            row = tile("u%d" % t, [P, S], F32)
+            if t < DIRECT:
+                nc.scalar.activation(row[:], acc[:], ACT.Sigmoid)
+            else:
+                nc.scalar.copy(row[:], acc[:])
+            u_rows.append(row)
+
+        idx_w = pick("idx_w", xw[:].bitcast(U32), U32, offs_t)
+        w1d = deal("w1d", w1w, I32, 4)
+        y_rows = []
+        for t in range(PACK):
+            acc = project(t, PACK + t, w1d, 4, idx_w, idx_s)
+            row = tile("y%d" % t, [P, S], F32)
+            nc.scalar.copy(row[:], acc[:])
+            y_rows.append(row)
+
+        for t in range(DIRECT):
+            nc.vector.tensor_copy(c_a[:, t, :], u_rows[t][:].indirect(ba_t[:]))
+            nc.vector.tensor_copy(c_b[:, t, :], u_rows[t][:].indirect(bb_t[:]))
+        w3d = deal("w3d", w3w, I32, 4)
+        w3sd = deal("w3sd", w3s, U8, 16)
+
+        y_a = tile("y_a", [P, PACK, V], F32)
+        dy = tile("dy", [P, PACK, V], F32)
+        gap = tile("gap", [P, PACK, V], F32)
+        for t in range(PACK):
+            nc.vector.tensor_copy(y_a[:, t, :], y_rows[t][:].indirect(ba_t[:]))
+            nc.vector.tensor_tensor(dy[:, t, :], y_rows[t][:].indirect(bb_t[:]), y_a[:, t, :], ALU.subtract)
+            if t >= DIRECT:
+                nc.scalar.activation(c_a[:, t, :], u_rows[t][:].indirect(ba_t[:]), ACT.Sigmoid)
+                nc.scalar.activation(c_b[:, t, :], u_rows[t][:].indirect(bb_t[:]), ACT.Sigmoid)
+            if t % 2 == 1:
+                nc.scalar.activation(gap[:, t - 1 : t + 1, :], dy[:, t - 1 : t + 1, :], ACT.Abs, scale=0.5)
+
+        both = tile("both", [P, PACK, V], F32)
+        least = tile("least", [P, PACK, V], F32)
+        reach = tile("reach", [P, PACK, V], F32)
+        share = tile("share", [P, PACK, V], F32)
+        for g in range(2):
+            ts = slice(2 * g, 2 * g + 2)
+            nc.vector.tensor_tensor(both[:, ts, :], c_a[:, ts, :], c_b[:, ts, :], ALU.add)
+            nc.vector.tensor_tensor(least[:, ts, :], c_a[:, ts, :], c_b[:, ts, :], ALU.min)
+            nc.vector.scalar_tensor_tensor(reach[:, ts, :], both[:, ts, :], 0.5, gap[:, ts, :], ALU.mult, ALU.subtract)
+            nc.vector.scalar_tensor_tensor(share[:, ts, :], reach[:, ts, :], 0.0, least[:, ts, :], ALU.max, ALU.min)
+
+        cover = tile("cover", [P, PACK, V], F32)
+        root = tile("root", [P, PACK, V], F32)
+        inv = tile("inv", [P, PACK, V], F32)
+        z_rows = tile("z_rows", [P, PACK, V], BF16)
+        z_in = tile("z_in", [P, V, PACK], BF16)
+        z_w = tile("z_w", [P, V], U32)
+        z_s = tile("z_s", [P, V], U8)
+        o_rows = tile("o_rows", [P, PACK, V], F32)
+        o_in = tile("o_in", [P, V, PACK], BF16)
+        o_w = tile("o_w", [P, V], I32)
+        o_s = tile("o_s", [P, V], U8)
+        halves = [slice(h * HALF, (h + 1) * HALF) for h in range(2)]
+
+        def weave(engine_copy, dst, src, vs):
+            engine_copy(dst[:, vs, :].rearrange("p (c i) t -> p c t i", i=4), src[:, :, vs].rearrange("p t (c i) -> p c t i", i=4))
+
+        for vs in halves:
+            nc.vector.scalar_tensor_tensor(cover[:, :, vs], both[:, :, vs], 0.05, share[:, :, vs], ALU.add, ALU.subtract)
+            nc.scalar.activation(root[:, :, vs], cover[:, :, vs], ACT.Abs_reciprocal_sqrt)
+            nc.scalar.activation(inv[:, :, vs], root[:, :, vs], ACT.Square)
+        out_rows = out_0.rearrange("(p t) v -> p t v", t=PACK)
+        for h, vs in enumerate(halves):
+            for t in range(PACK):
+                nc.vector.scalar_tensor_tensor(z_rows[:, t, vs], inv[:, t, vs], gain[:, t : t + 1], share[:, t, vs], ALU.mult, ALU.mult)
+            weave(nc.vector.tensor_copy, z_in, z_rows, vs)
+            nc.vector.quantize_mx(out=z_w[:, vs].bitcast(FP8X4), scales=z_s[:, vs], in_=z_in[:, vs, :].rearrange("p v t -> p (v t)"))
+            acc = psum.tile([P, PACK, HALF], F32, name="last%d" % h, tag="bank%d" % h)
+            for t in range(PACK):
+                cols = slice(t * P, (t + 1) * P)
+                nc.tensor.matmul_mx(out=acc[:, t, :], lhsT=w3d[:, cols].bitcast(FP8X4), lhsT_scale=w3sd[:, cols],
+                                    rhs=z_w[:, vs].bitcast(FP8X4), rhs_scale=z_s[:, vs], start=True, stop=True)
+            nc.vector.tensor_tensor(o_rows[:, :, vs], acc[:], resid[:, :, vs], ALU.add)
+            nc.sync.dma_start(out_rows[:, :, vs], o_rows[:, :, vs])
+            weave(nc.scalar.copy, o_in, o_rows, vs)
+            nc.vector.quantize_mx(out=o_w[:, vs].bitcast(FP8X4), scales=o_s[:, vs], in_=o_in[:, vs, :].rearrange("p v t -> p (v t)"))
+        nc.sync.dma_start(out_1[0].rearrange("p n t -> p (n t)").bitcast(I32), o_w[:])
+        for q in range(4):
+            queue = nc.scalar if q % 2 else nc.sync
+            queue.dma_start(out_2[0, 4 * q : 4 * q + 4, :].bitcast(I32), o_s[32 * q : 32 * q + 4, :].bitcast(I32))

@@ -18,7 +18,7 @@ ACT = mybir.ActivationFunctionType
 P = 128
 PACK = 4
 HALF = V // 2
-DIRECT = 1
+DIRECT = 0
 
 
 def tile_picked_boxiou_none_po_kernel(tc, x_words, x_scales, w1_words, w1_scales, w2_words, w2_scales, gn, w3_words, w3_scales, res, offs, two, ba, bb, out_0, out_1, out_2):
@@ -27,16 +27,16 @@ def tile_picked_boxiou_none_po_kernel(tc, x_words, x_scales, w1_words, w1_scales
         keep = ctx.enter_context(tc.tile_pool(name="keep", bufs=1))
         psum = ctx.enter_context(tc.psum_pool(name="psum", bufs=1))
 
-        def tile(name, shape, dtype):
-            return keep.tile(shape, dtype, name=name, align_bytes=64)
+        def tile(name, shape, dtype, tag=None):
+            return keep.tile(shape, dtype, name=name, tag=tag or name, align_bytes=64)
 
         def load_list(name, src):
             dst = tile(name, list(src.shape), U16)
             nc.sync.dma_start(dst[:], src)
             return dst
 
-        def load_words(queue, name, src):
-            dst = tile(name, [P, src.shape[2]], I32)
+        def load_words(queue, name, src, tag=None):
+            dst = tile(name, [P, src.shape[2]], I32, tag)
             queue.dma_start(dst[:], src[0].rearrange("p n t -> p (n t)").bitcast(I32))
             return dst
 
@@ -44,9 +44,9 @@ def tile_picked_boxiou_none_po_kernel(tc, x_words, x_scales, w1_words, w1_scales
             for q in range(4):
                 queue.dma_start(dst[32 * q + first : 32 * q + first + 4, :].bitcast(I32), src[0, 4 * q : 4 * q + 4, :].bitcast(I32))
 
-        def deal(name, src, dtype, run):
-            dst = tile(name, [P, PACK * P], dtype)
-            nc.vector.tensor_copy(
+        def deal(engine, name, src, dtype, run, tag=None):
+            dst = tile(name, [P, PACK * P], dtype, tag)
+            engine.tensor_copy(
                 dst[:].rearrange("p (t c i) -> p c t i", t=PACK, i=run),
                 src[:].rearrange("p (c i t) -> p c t i", t=PACK, i=run),
             )
@@ -54,27 +54,25 @@ def tile_picked_boxiou_none_po_kernel(tc, x_words, x_scales, w1_words, w1_scales
 
         xs = tile("xs", [P, T], U8)
         nc.vector.memset(xs[:].bitcast(I32), 0)
+        w2s = tile("w2s", [P, H], U8)
+        nc.gpsimd.memset(w2s[:].bitcast(I32), 0)
         ws = tile("ws", [P, H], U8)
-        nc.vector.memset(ws[:].bitcast(I32), 0)
-        w3s = tile("w3s", [P, N], U8)
-        nc.vector.memset(w3s[:].bitcast(I32), 0)
-
+        nc.gpsimd.memset(ws[:].bitcast(I32), 0)
         two_t = load_list("two_t", two)
-        load_scales(nc.sync, xs, 0, x_scales)
-        offs_t = load_list("offs_t", offs)
+        load_scales(nc.scalar, xs, 0, x_scales)
         xw = load_words(nc.sync, "xw", x_words)
         w2w = load_words(nc.sync, "w2w", w2_words)
-        load_scales(nc.sync, ws, 0, w2_scales)
-        load_scales(nc.scalar, ws, 4, w1_scales)
+        load_scales(nc.sync, w2s, 0, w2_scales)
+        offs_t = load_list("offs_t", offs)
+        load_scales(nc.sync, ws, 0, w1_scales)
+        load_scales(nc.gpsimd, ws, 4, w3_scales)
         w1w = load_words(nc.sync, "w1w", w1_words)
         ba_t = load_list("ba_t", ba)
         bb_t = load_list("bb_t", bb)
-        w3w = load_words(nc.sync, "w3w", w3_words)
-        load_scales(nc.sync, w3s, 0, w3_scales)
-        gain = tile("gain", [P, PACK], F32)
-        nc.sync.dma_start(gain[:], gn.rearrange("(p t) o -> p (t o)", t=PACK))
-        resid = tile("resid", [P, PACK, V], F32)
-        nc.sync.dma_start(resid[:], res.rearrange("(p t) v -> p t v", t=PACK))
+
+        warm = tile("warm", [P, 2], F32)
+        nc.vector.memset(warm[:, 0:1], 0.0)
+        nc.scalar.activation(warm[:, 1:2], warm[:, 0:1], ACT.Sigmoid)
 
         def pick(name, window, dtype, lst):
             dst = tile(name, [P, S], dtype)
@@ -82,104 +80,148 @@ def tile_picked_boxiou_none_po_kernel(tc, x_words, x_scales, w1_words, w1_scales
             return dst
 
         two_s = pick("two_s", xs[:], U8, two_t)
-        idx_s = pick("idx_s", xs[:], U8, offs_t)
         two_w = pick("two_w", xw[:].bitcast(U32), U32, two_t)
-        w2d = deal("w2d", w2w, I32, 4)
-        wsd = deal("wsd", ws, U8, 16)
+        w2d = deal(nc.vector, "w2d", w2w, I32, 4)
+        w2sd = deal(nc.vector, "w2sd", w2s, U8, 16)
+        w3w = load_words(nc.sync, "w3w", w3_words, "w2w")
 
-        def project(t, bank, wd, first, xw_p, xs_p):
+        def project(t, bank, wd, sd, xw_p, xs_p):
             acc = psum.tile([P, S], F32, name="acc%d" % bank, tag="bank%d" % bank)
             cols = slice(t * P, (t + 1) * P)
-            nc.tensor.matmul_mx(out=acc[:], lhsT=wd[:, cols].bitcast(FP8X4), lhsT_scale=wsd[first:P, cols],
+            nc.tensor.matmul_mx(out=acc[:], lhsT=wd[:, cols].bitcast(FP8X4), lhsT_scale=sd[:, cols],
                                 rhs=xw_p[:].bitcast(FP8X4), rhs_scale=xs_p[:], start=True, stop=True)
             return acc
 
+        halves = [slice(h * HALF, (h + 1) * HALF) for h in range(2)]
+        pairs = [slice(0, 2), slice(2, 4)]
         c_a = tile("c_a", [P, PACK, V], F32)
         c_b = tile("c_b", [P, PACK, V], F32)
-        u_rows = []
-        for t in range(PACK):
-            acc = project(t, t, w2d, 0, two_w, two_s)
-            row = tile("u%d" % t, [P, S], F32)
-            if t < DIRECT:
-                nc.scalar.activation(row[:], acc[:], ACT.Sigmoid)
-            else:
-                nc.scalar.copy(row[:], acc[:])
-            u_rows.append(row)
-
-        idx_w = pick("idx_w", xw[:].bitcast(U32), U32, offs_t)
-        w1d = deal("w1d", w1w, I32, 4)
-        y_rows = []
-        for t in range(PACK):
-            acc = project(t, PACK + t, w1d, 4, idx_w, idx_s)
-            row = tile("y%d" % t, [P, S], F32)
-            nc.scalar.copy(row[:], acc[:])
-            y_rows.append(row)
-
-        for t in range(DIRECT):
-            nc.vector.tensor_copy(c_a[:, t, :], u_rows[t][:].indirect(ba_t[:]))
-            nc.vector.tensor_copy(c_b[:, t, :], u_rows[t][:].indirect(bb_t[:]))
-        w3d = deal("w3d", w3w, I32, 4)
-        w3sd = deal("w3sd", w3s, U8, 16)
-
         y_a = tile("y_a", [P, PACK, V], F32)
         dy = tile("dy", [P, PACK, V], F32)
         gap = tile("gap", [P, PACK, V], F32)
-        for t in range(PACK):
-            nc.vector.tensor_copy(y_a[:, t, :], y_rows[t][:].indirect(ba_t[:]))
-            nc.vector.tensor_tensor(dy[:, t, :], y_rows[t][:].indirect(bb_t[:]), y_a[:, t, :], ALU.subtract)
-            if t >= DIRECT:
-                nc.scalar.activation(c_a[:, t, :], u_rows[t][:].indirect(ba_t[:]), ACT.Sigmoid)
-                nc.scalar.activation(c_b[:, t, :], u_rows[t][:].indirect(bb_t[:]), ACT.Sigmoid)
-            if t % 2 == 1:
-                nc.scalar.activation(gap[:, t - 1 : t + 1, :], dy[:, t - 1 : t + 1, :], ACT.Abs, scale=0.5)
 
-        both = tile("both", [P, PACK, V], F32)
-        least = tile("least", [P, PACK, V], F32)
-        reach = tile("reach", [P, PACK, V], F32)
-        share = tile("share", [P, PACK, V], F32)
-        for g in range(2):
-            ts = slice(2 * g, 2 * g + 2)
+        u_acc = [project(t, t, w2d, w2sd, two_w, two_s) for t in range(2)]
+
+        def widths(t):
+            row = tile("u%d" % t, [P, S], F32)
+            if t < DIRECT:
+                nc.scalar.activation(row[:], u_acc[t][:], ACT.Sigmoid)
+                nc.vector.tensor_copy(c_a[:, t, :], row[:].indirect(ba_t[:]))
+                nc.vector.tensor_copy(c_b[:, t, :], row[:].indirect(bb_t[:]))
+            else:
+                nc.scalar.copy(row[:], u_acc[t][:])
+                nc.scalar.activation(c_a[:, t, :], row[:].indirect(ba_t[:]), ACT.Sigmoid)
+                nc.scalar.activation(c_b[:, t, :], row[:].indirect(bb_t[:]), ACT.Sigmoid)
+
+        def combine(ts):
             nc.vector.tensor_tensor(both[:, ts, :], c_a[:, ts, :], c_b[:, ts, :], ALU.add)
             nc.vector.tensor_tensor(least[:, ts, :], c_a[:, ts, :], c_b[:, ts, :], ALU.min)
-            nc.vector.scalar_tensor_tensor(reach[:, ts, :], both[:, ts, :], 0.5, gap[:, ts, :], ALU.mult, ALU.subtract)
-            nc.vector.scalar_tensor_tensor(share[:, ts, :], reach[:, ts, :], 0.0, least[:, ts, :], ALU.max, ALU.min)
 
-        cover = tile("cover", [P, PACK, V], F32)
-        root = tile("root", [P, PACK, V], F32)
-        inv = tile("inv", [P, PACK, V], F32)
-        z_rows = tile("z_rows", [P, PACK, V], BF16)
-        z_in = tile("z_in", [P, V, PACK], BF16)
-        z_w = tile("z_w", [P, V], U32)
-        z_s = tile("z_s", [P, V], U8)
-        o_rows = tile("o_rows", [P, PACK, V], F32)
-        o_in = tile("o_in", [P, V, PACK], BF16)
-        o_w = tile("o_w", [P, V], I32)
-        o_s = tile("o_s", [P, V], U8)
-        halves = [slice(h * HALF, (h + 1) * HALF) for h in range(2)]
+        def middles(t):
+            row = tile("y%d" % t, [P, S], F32)
+            nc.scalar.copy(row[:], y_acc[t][:])
+            return row
 
-        def weave(engine_copy, dst, src, vs):
-            engine_copy(dst[:, vs, :].rearrange("p (c i) t -> p c t i", i=4), src[:, :, vs].rearrange("p t (c i) -> p c t i", i=4))
+        def first_middle(t):
+            nc.vector.tensor_copy(y_a[:, t, :], y_rows[t][:].indirect(ba_t[:]))
 
-        for vs in halves:
-            nc.vector.scalar_tensor_tensor(cover[:, :, vs], both[:, :, vs], 0.05, share[:, :, vs], ALU.add, ALU.subtract)
-            nc.scalar.activation(root[:, :, vs], cover[:, :, vs], ACT.Abs_reciprocal_sqrt)
-            nc.scalar.activation(inv[:, :, vs], root[:, :, vs], ACT.Square)
+        def distance(t):
+            nc.vector.tensor_tensor(dy[:, t, :], y_rows[t][:].indirect(bb_t[:]), y_a[:, t, :], ALU.subtract)
+
+        def halve(ts):
+            nc.scalar.activation(gap[:, ts, :], dy[:, ts, :], ACT.Abs, scale=0.5)
+
+        idx_s = pick("idx_s", xs[:], U8, offs_t)
+        resid = tile("resid", [P, PACK, V], F32, "xs")
+        nc.sync.dma_start(resid[:], res.rearrange("(p t) v -> p t v", t=PACK))
+        idx_w = pick("idx_w", xw[:].bitcast(U32), U32, offs_t)
+        w1d = deal(nc.vector, "w1d", w1w, I32, 4)
+        wsd = deal(nc.vector, "wsd", ws, U8, 16, "w2s")
+        y_acc = [project(t, PACK + t, w1d, wsd, idx_w, idx_s) for t in range(PACK)]
+        w3d = deal(nc.vector, "w3d", w3w, I32, 4)
+        both = tile("both", [P, PACK, V], F32, tag="w1w")
+        least = tile("least", [P, PACK, V], F32, tag="ws")
+        y_rows = []
+        widths(0)
+        widths(1)
+        y_rows.append(middles(0))
+        combine(pairs[0])
+        y_rows.append(middles(1))
+        first_middle(0)
+        first_middle(1)
+        u_acc.append(project(2, PACK, w2d, w2sd, two_w, two_s))
+        widths(2)
+        distance(0)
+        y_rows.append(middles(2))
+        distance(1)
+        y_rows.append(middles(3))
+        first_middle(2)
+        u_acc.append(project(3, PACK + 2, w2d, w2sd, two_w, two_s))
+        widths(3)
+        first_middle(3)
+        halve(pairs[0])
+        distance(2)
+        distance(3)
+        halve(pairs[1])
+        combine(pairs[1])
+
+        gain = tile("gain", [P, PACK], F32, "two_s")
+        nc.sync.dma_start(gain[:], gn.rearrange("(p t) o -> p (t o)", t=PACK))
         out_rows = out_0.rearrange("(p t) v -> p t v", t=PACK)
+        out_words = out_1[0].rearrange("p n t -> p (n t)").bitcast(I32)
+        o_s = tile("o_s", [P, V], U8)
+
+        def weave(engine_copy, name, src):
+            dst = tile(name, [P, HALF * PACK], BF16)
+            engine_copy(dst[:].rearrange("p (c i t) -> p c t i", i=4, t=PACK), src[:].rearrange("p t (c i) -> p c t i", i=4))
+            return dst
+
+        share, inv = [], []
         for h, vs in enumerate(halves):
+            reach = tile("reach%d" % h, [P, PACK, HALF], F32)
+            sh = tile("share%d" % h, [P, PACK, HALF], F32)
+            cover = tile("cover%d" % h, [P, PACK, HALF], F32)
+            root = tile("root%d" % h, [P, PACK, HALF], F32)
+            iv = tile("inv%d" % h, [P, PACK, HALF], F32)
+            for ts in pairs:
+                nc.vector.scalar_tensor_tensor(reach[:, ts, :], both[:, ts, vs], 0.5, gap[:, ts, vs], ALU.mult, ALU.subtract)
+            for ts in pairs:
+                nc.vector.scalar_tensor_tensor(sh[:, ts, :], reach[:, ts, :], 0.0, least[:, ts, vs], ALU.max, ALU.min)
+            for ts in pairs:
+                nc.vector.scalar_tensor_tensor(cover[:, ts, :], both[:, ts, vs], 0.05, sh[:, ts, :], ALU.add, ALU.subtract)
+            nc.scalar.activation(root[:], cover[:], ACT.Abs_reciprocal_sqrt)
+            nc.scalar.activation(iv[:], root[:], ACT.Square)
+            share.append(sh)
+            inv.append(iv)
+
+        accs = []
+        for h in range(2):
+            z_rows = tile("z_rows%d" % h, [P, PACK, HALF], BF16)
             for t in range(PACK):
-                nc.vector.scalar_tensor_tensor(z_rows[:, t, vs], inv[:, t, vs], gain[:, t : t + 1], share[:, t, vs], ALU.mult, ALU.mult)
-            weave(nc.vector.tensor_copy, z_in, z_rows, vs)
-            nc.vector.quantize_mx(out=z_w[:, vs].bitcast(FP8X4), scales=z_s[:, vs], in_=z_in[:, vs, :].rearrange("p v t -> p (v t)"))
-            acc = psum.tile([P, PACK, HALF], F32, name="last%d" % h, tag="bank%d" % h)
-            for t in range(PACK):
-                cols = slice(t * P, (t + 1) * P)
-                nc.tensor.matmul_mx(out=acc[:, t, :], lhsT=w3d[:, cols].bitcast(FP8X4), lhsT_scale=w3sd[:, cols],
-                                    rhs=z_w[:, vs].bitcast(FP8X4), rhs_scale=z_s[:, vs], start=True, stop=True)
-            nc.vector.tensor_tensor(o_rows[:, :, vs], acc[:], resid[:, :, vs], ALU.add)
-            nc.sync.dma_start(out_rows[:, :, vs], o_rows[:, :, vs])
-            weave(nc.scalar.copy, o_in, o_rows, vs)
-            nc.vector.quantize_mx(out=o_w[:, vs].bitcast(FP8X4), scales=o_s[:, vs], in_=o_in[:, vs, :].rearrange("p v t -> p (v t)"))
-        nc.sync.dma_start(out_1[0].rearrange("p n t -> p (n t)").bitcast(I32), o_w[:])
+                nc.vector.scalar_tensor_tensor(z_rows[:, t, :], inv[h][:, t, :], gain[:, t : t + 1], share[h][:, t, :], ALU.mult, ALU.mult)
+            z_in = weave(nc.vector.tensor_copy, "z_in%d" % h, z_rows)
+            z_w = tile("z_w%d" % h, [P, HALF], U32)
+            z_s = tile("z_s%d" % h, [P, HALF], U8)
+            nc.vector.quantize_mx(out=z_w[:].bitcast(FP8X4), scales=z_s[:], in_=z_in[:])
+            for g, ts in enumerate(pairs):
+                acc = psum.tile([P, 2, HALF], F32, name="last%d%d" % (h, g), tag="bank%d" % (2 * h + g))
+                for t in range(ts.start, ts.stop):
+                    cols = slice(t * P, (t + 1) * P)
+                    nc.tensor.matmul_mx(out=acc[:, t - ts.start, :], lhsT=w3d[:, cols].bitcast(FP8X4), lhsT_scale=wsd[4:P, cols],
+                                        rhs=z_w[:].bitcast(FP8X4), rhs_scale=z_s[:], start=True, stop=True)
+                accs.append(acc)
+        copies = [nc.scalar.copy, nc.vector.tensor_copy]
+        o_in = []
+        for h, vs in enumerate(halves):
+            o_rows = tile("o_rows%d" % h, [P, PACK, HALF], F32)
+            for g, ts in enumerate(pairs):
+                nc.vector.tensor_tensor(o_rows[:, ts, :], accs[2 * h + g][:], resid[:, ts, vs], ALU.add)
+            nc.sync.dma_start(out_rows[:, :, vs], o_rows[:])
+            o_in.append(weave(copies[h], "o_in%d" % h, o_rows))
+        for h, vs in enumerate(halves):
+            o_w = tile("o_w%d" % h, [P, HALF], I32)
+            nc.vector.quantize_mx(out=o_w[:].bitcast(FP8X4), scales=o_s[:, vs], in_=o_in[h][:])
+            nc.sync.dma_start(out_words[:, vs], o_w[:])
         for q in range(4):
             queue = nc.scalar if q % 2 else nc.sync
             queue.dma_start(out_2[0, 4 * q : 4 * q + 4, :].bitcast(I32), o_s[32 * q : 32 * q + 4, :].bitcast(I32))

@@ -17,211 +17,212 @@ ACT = mybir.ActivationFunctionType
 
 P = 128
 PACK = 4
+QUADRANTS = 4
+LINE = 16
 HALF = V // 2
-DIRECT = 0
+HALVES = [slice(0, HALF), slice(HALF, V)]
+TILE_PAIRS = [slice(0, 2), slice(2, 4)]
 
 
-def tile_picked_boxiou_none_po_kernel(tc, x_words, x_scales, w1_words, w1_scales, w2_words, w2_scales, gn, w3_words, w3_scales, res, offs, two, ba, bb, out_0, out_1, out_2):
+def tile_picked_boxiou_none_po_kernel(
+    tc, x_words, x_scales, w1_words, w1_scales, w2_words, w2_scales, gn, w3_words, w3_scales, res, offs, two, ba, bb, out_0, out_1, out_2
+):
     nc = tc.nc
     with ExitStack() as ctx:
         keep = ctx.enter_context(tc.tile_pool(name="keep", bufs=1))
         psum = ctx.enter_context(tc.psum_pool(name="psum", bufs=1))
 
-        def tile(name, shape, dtype, tag=None):
-            return keep.tile(shape, dtype, name=name, tag=tag or name, align_bytes=64)
+        def tile(name, shape, dtype, after=None):
+            return keep.tile(shape, dtype, name=name, tag=after or name, align_bytes=64)
 
         def load_list(name, src):
             dst = tile(name, list(src.shape), U16)
             nc.sync.dma_start(dst[:], src)
             return dst
 
-        def load_words(queue, name, src, tag=None):
-            dst = tile(name, [P, src.shape[2]], I32, tag)
-            queue.dma_start(dst[:], src[0].rearrange("p n t -> p (n t)").bitcast(I32))
+        def load_words(name, src, after=None):
+            dst = tile(name, [P, src.shape[2]], I32, after)
+            nc.sync.dma_start(dst[:], src[0].rearrange("p n t -> p (n t)").bitcast(I32))
             return dst
 
-        def load_scales(queue, dst, first, src):
-            for q in range(4):
-                queue.dma_start(dst[32 * q + first : 32 * q + first + 4, :].bitcast(I32), src[0, 4 * q : 4 * q + 4, :].bitcast(I32))
+        def load_scales(queue, dst, src, quadrants=range(QUADRANTS)):
+            for q in quadrants:
+                queue.dma_start(dst[32 * q : 32 * q + 4, :].bitcast(I32), src[0, 4 * q : 4 * q + 4, :].bitcast(I32))
 
-        def deal(engine, name, src, dtype, run, tag=None):
-            dst = tile(name, [P, PACK * P], dtype, tag)
-            engine.tensor_copy(
+        def deal(name, src, dtype, run, after=None):
+            dst = tile(name, [P, PACK * P], dtype, after)
+            nc.gpsimd.tensor_copy(
                 dst[:].rearrange("p (t c i) -> p c t i", t=PACK, i=run),
                 src[:].rearrange("p (c i t) -> p c t i", t=PACK, i=run),
             )
             return dst
 
-        xs = tile("xs", [P, T], U8)
-        nc.vector.memset(xs[:].bitcast(I32), 0)
-        w2s = tile("w2s", [P, H], U8)
-        nc.gpsimd.memset(w2s[:].bitcast(I32), 0)
-        ws = tile("ws", [P, H], U8)
-        nc.gpsimd.memset(ws[:].bitcast(I32), 0)
-        two_t = load_list("two_t", two)
-        load_scales(nc.scalar, xs, 0, x_scales)
-        xw = load_words(nc.sync, "xw", x_words)
-        w2w = load_words(nc.sync, "w2w", w2_words)
-        load_scales(nc.sync, w2s, 0, w2_scales)
-        offs_t = load_list("offs_t", offs)
-        load_scales(nc.sync, ws, 0, w1_scales)
-        load_scales(nc.gpsimd, ws, 4, w3_scales)
-        w1w = load_words(nc.sync, "w1w", w1_words)
-        ba_t = load_list("ba_t", ba)
-        bb_t = load_list("bb_t", bb)
-
-        warm = tile("warm", [P, 2], F32)
-        nc.vector.memset(warm[:, 0:1], 0.0)
-        nc.scalar.activation(warm[:, 1:2], warm[:, 0:1], ACT.Sigmoid)
-
-        def pick(name, window, dtype, lst):
+        def pick(name, window, dtype, offsets):
             dst = tile(name, [P, S], dtype)
-            nc.vector.tensor_copy(dst[:], window.indirect(lst[:]))
+            nc.vector.tensor_copy(dst[:], window.indirect(offsets[:]))
             return dst
 
-        two_s = pick("two_s", xs[:], U8, two_t)
-        two_w = pick("two_w", xw[:].bitcast(U32), U32, two_t)
-        w2d = deal(nc.vector, "w2d", w2w, I32, 4)
-        w2sd = deal(nc.vector, "w2sd", w2s, U8, 16)
-        w3w = load_words(nc.sync, "w3w", w3_words, "w2w")
+        x_sc = tile("x_sc", [P, T], U8)
+        nc.vector.memset(x_sc[:, : T // 2].bitcast(I32), 0)
+        nc.gpsimd.memset(x_sc[:, T // 2 :].bitcast(I32), 0)
+        w2_sc = tile("w2_sc", [P, H], U8)
+        nc.gpsimd.memset(w2_sc[:].bitcast(I32), 0)
+        w1_sc = tile("w1_sc", [P, H], U8)
+        nc.gpsimd.memset(w1_sc[:].bitcast(I32), 0)
 
-        def project(t, bank, wd, sd, xw_p, xs_p):
+        load_scales(nc.gpsimd, w1_sc, w1_scales, range(QUADRANTS // 2, QUADRANTS))
+        two_list = load_list("two_list", two)
+        load_scales(nc.sync, x_sc, x_scales)
+        idx_list = load_list("idx_list", offs)
+        x_wd = load_words("x_wd", x_words)
+        w2_wd = load_words("w2_wd", w2_words)
+        load_scales(nc.sync, w2_sc, w2_scales)
+        w1_wd = load_words("w1_wd", w1_words)
+        load_scales(nc.sync, w1_sc, w1_scales, range(QUADRANTS // 2))
+        ba_list = load_list("ba_list", ba)
+        bb_list = load_list("bb_list", bb)
+
+        two_sc = pick("two_sc", x_sc[:], U8, two_list)
+        idx_sc = pick("idx_sc", x_sc[:], U8, idx_list)
+        resid = tile("resid", [P, PACK, V], F32, "x_sc")
+        nc.sync.dma_start(resid[:], res.rearrange("(p t) v -> p t v", t=PACK))
+        two_wd = pick("two_wd", x_wd[:].bitcast(U32), U32, two_list)
+        w2_dealt = deal("w2_dealt", w2_wd, I32, LINE // 4)
+        w2_sc_dealt = deal("w2_sc_dealt", w2_sc, U8, LINE)
+        w3_wd = load_words("w3_wd", w3_words, "w2_wd")
+
+        def project(t, bank, words, scales, picked_words, picked_scales):
             acc = psum.tile([P, S], F32, name="acc%d" % bank, tag="bank%d" % bank)
             cols = slice(t * P, (t + 1) * P)
-            nc.tensor.matmul_mx(out=acc[:], lhsT=wd[:, cols].bitcast(FP8X4), lhsT_scale=sd[:, cols],
-                                rhs=xw_p[:].bitcast(FP8X4), rhs_scale=xs_p[:], start=True, stop=True)
+            nc.tensor.matmul_mx(
+                out=acc[:], lhsT=words[:, cols].bitcast(FP8X4), lhsT_scale=scales[:, cols],
+                rhs=picked_words[:].bitcast(FP8X4), rhs_scale=picked_scales[:], start=True, stop=True,
+            )
             return acc
 
-        halves = [slice(h * HALF, (h + 1) * HALF) for h in range(2)]
-        pairs = [slice(0, 2), slice(2, 4)]
+        def project_logits(t, bank):
+            return project(t, bank, w2_dealt, w2_sc_dealt, two_wd, two_sc)
+
+        def unload(name, acc):
+            row = tile(name, [P, S], F32)
+            nc.scalar.copy(row[:], acc[:])
+            return row
+
         c_a = tile("c_a", [P, PACK, V], F32)
         c_b = tile("c_b", [P, PACK, V], F32)
         y_a = tile("y_a", [P, PACK, V], F32)
-        dy = tile("dy", [P, PACK, V], F32)
+        y_diff = tile("y_diff", [P, PACK, V], F32)
         gap = tile("gap", [P, PACK, V], F32)
 
-        u_acc = [project(t, t, w2d, w2sd, two_w, two_s) for t in range(2)]
+        def widths_on_scalar(t, logits):
+            nc.scalar.activation(c_a[:, t, :], logits[:].indirect(ba_list[:]), ACT.Sigmoid)
+            nc.scalar.activation(c_b[:, t, :], logits[:].indirect(bb_list[:]), ACT.Sigmoid)
 
-        def widths(t):
-            row = tile("u%d" % t, [P, S], F32)
-            if t < DIRECT:
-                nc.scalar.activation(row[:], u_acc[t][:], ACT.Sigmoid)
-                nc.vector.tensor_copy(c_a[:, t, :], row[:].indirect(ba_t[:]))
-                nc.vector.tensor_copy(c_b[:, t, :], row[:].indirect(bb_t[:]))
-            else:
-                nc.scalar.copy(row[:], u_acc[t][:])
-                nc.scalar.activation(c_a[:, t, :], row[:].indirect(ba_t[:]), ACT.Sigmoid)
-                nc.scalar.activation(c_b[:, t, :], row[:].indirect(bb_t[:]), ACT.Sigmoid)
+        def middles_a(ts):
+            for t in range(ts.start, ts.stop):
+                nc.vector.tensor_copy(y_a[:, t, :], y_rows[t][:].indirect(ba_list[:]))
 
-        def combine(ts):
+        def middles_b_minus_a(ts):
+            for t in range(ts.start, ts.stop):
+                nc.vector.tensor_tensor(y_diff[:, t, :], y_rows[t][:].indirect(bb_list[:]), y_a[:, t, :], ALU.subtract)
+
+        def half_distance(ts):
+            nc.scalar.activation(gap[:, ts, :], y_diff[:, ts, :], ACT.Abs, scale=0.5)
+
+        logit_acc = [project_logits(t, t) for t in range(2)]
+        idx_wd = pick("idx_wd", x_wd[:].bitcast(U32), U32, idx_list)
+        w1_dealt = deal("w1_dealt", w1_wd, I32, LINE // 4)
+        w1_sc_dealt = deal("w1_sc_dealt", w1_sc, U8, LINE, "w2_sc")
+        y_acc = [project(t, PACK + t, w1_dealt, w1_sc_dealt, idx_wd, idx_sc) for t in range(PACK)]
+        w3_dealt = deal("w3_dealt", w3_wd, I32, LINE // 4)
+        w3_sc = tile("w3_sc", [P, N], U8, "idx_sc")
+        nc.gpsimd.memset(w3_sc[:].bitcast(I32), 0)
+        load_scales(nc.sync, w3_sc, w3_scales)
+        w3_sc_dealt = deal("w3_sc_dealt", w3_sc, U8, LINE)
+        both = tile("both", [P, PACK, V], F32, "w1_wd")
+        least = tile("least", [P, PACK, V], F32, "w1_sc")
+
+        low, high = TILE_PAIRS
+        c_row = tile("c_row", [P, S], F32)
+        nc.scalar.activation(c_row[:], logit_acc[0][:], ACT.Sigmoid)
+        nc.vector.tensor_copy(c_a[:, 0, :], c_row[:].indirect(ba_list[:]))
+        nc.vector.tensor_copy(c_b[:, 0, :], c_row[:].indirect(bb_list[:]))
+        logits_1 = unload("logits_1", logit_acc[1])
+        y_rows = [unload("y_row%d" % t, y_acc[t]) for t in range(low.start, low.stop)]
+        middles_a(low)
+        widths_on_scalar(1, logits_1)
+        middles_b_minus_a(low)
+        y_rows.extend(unload("y_row%d" % t, y_acc[t]) for t in range(high.start, high.stop))
+        widths_on_scalar(2, unload("logits_2", project_logits(2, PACK + low.start)))
+        middles_a(high)
+        widths_on_scalar(3, unload("logits_3", project_logits(3, PACK + high.start)))
+        half_distance(low)
+        middles_b_minus_a(high)
+        half_distance(high)
+        for ts in TILE_PAIRS:
             nc.vector.tensor_tensor(both[:, ts, :], c_a[:, ts, :], c_b[:, ts, :], ALU.add)
             nc.vector.tensor_tensor(least[:, ts, :], c_a[:, ts, :], c_b[:, ts, :], ALU.min)
 
-        def middles(t):
-            row = tile("y%d" % t, [P, S], F32)
-            nc.scalar.copy(row[:], y_acc[t][:])
-            return row
-
-        def first_middle(t):
-            nc.vector.tensor_copy(y_a[:, t, :], y_rows[t][:].indirect(ba_t[:]))
-
-        def distance(t):
-            nc.vector.tensor_tensor(dy[:, t, :], y_rows[t][:].indirect(bb_t[:]), y_a[:, t, :], ALU.subtract)
-
-        def halve(ts):
-            nc.scalar.activation(gap[:, ts, :], dy[:, ts, :], ACT.Abs, scale=0.5)
-
-        idx_s = pick("idx_s", xs[:], U8, offs_t)
-        resid = tile("resid", [P, PACK, V], F32, "xs")
-        nc.sync.dma_start(resid[:], res.rearrange("(p t) v -> p t v", t=PACK))
-        idx_w = pick("idx_w", xw[:].bitcast(U32), U32, offs_t)
-        w1d = deal(nc.vector, "w1d", w1w, I32, 4)
-        wsd = deal(nc.vector, "wsd", ws, U8, 16, "w2s")
-        y_acc = [project(t, PACK + t, w1d, wsd, idx_w, idx_s) for t in range(PACK)]
-        w3d = deal(nc.vector, "w3d", w3w, I32, 4)
-        both = tile("both", [P, PACK, V], F32, tag="w1w")
-        least = tile("least", [P, PACK, V], F32, tag="ws")
-        y_rows = []
-        widths(0)
-        widths(1)
-        y_rows.append(middles(0))
-        combine(pairs[0])
-        y_rows.append(middles(1))
-        first_middle(0)
-        first_middle(1)
-        u_acc.append(project(2, PACK, w2d, w2sd, two_w, two_s))
-        widths(2)
-        distance(0)
-        y_rows.append(middles(2))
-        distance(1)
-        y_rows.append(middles(3))
-        first_middle(2)
-        u_acc.append(project(3, PACK + 2, w2d, w2sd, two_w, two_s))
-        widths(3)
-        first_middle(3)
-        halve(pairs[0])
-        distance(2)
-        distance(3)
-        halve(pairs[1])
-        combine(pairs[1])
-
-        gain = tile("gain", [P, PACK], F32, "two_s")
+        gain = tile("gain", [P, PACK], F32, "two_sc")
         nc.sync.dma_start(gain[:], gn.rearrange("(p t) o -> p (t o)", t=PACK))
         out_rows = out_0.rearrange("(p t) v -> p t v", t=PACK)
         out_words = out_1[0].rearrange("p n t -> p (n t)").bitcast(I32)
-        o_s = tile("o_s", [P, V], U8)
+        out_sc = tile("out_sc", [P, V], U8)
 
-        def weave(engine_copy, name, src):
+        def weave(copy, name, src):
             dst = tile(name, [P, HALF * PACK], BF16)
-            engine_copy(dst[:].rearrange("p (c i t) -> p c t i", i=4, t=PACK), src[:].rearrange("p t (c i) -> p c t i", i=4))
+            copy(dst[:].rearrange("p (c i t) -> p c t i", i=4, t=PACK), src[:].rearrange("p t (c i) -> p c t i", i=4))
             return dst
 
-        share, inv = [], []
-        for h, vs in enumerate(halves):
+        shares, inverses = [], []
+        for h, vs in enumerate(HALVES):
             reach = tile("reach%d" % h, [P, PACK, HALF], F32)
-            sh = tile("share%d" % h, [P, PACK, HALF], F32)
+            share = tile("share%d" % h, [P, PACK, HALF], F32)
             cover = tile("cover%d" % h, [P, PACK, HALF], F32)
             root = tile("root%d" % h, [P, PACK, HALF], F32)
-            iv = tile("inv%d" % h, [P, PACK, HALF], F32)
-            for ts in pairs:
+            inverse = tile("inverse%d" % h, [P, PACK, HALF], F32)
+            for ts in TILE_PAIRS:
                 nc.vector.scalar_tensor_tensor(reach[:, ts, :], both[:, ts, vs], 0.5, gap[:, ts, vs], ALU.mult, ALU.subtract)
-            for ts in pairs:
-                nc.vector.scalar_tensor_tensor(sh[:, ts, :], reach[:, ts, :], 0.0, least[:, ts, vs], ALU.max, ALU.min)
-            for ts in pairs:
-                nc.vector.scalar_tensor_tensor(cover[:, ts, :], both[:, ts, vs], 0.05, sh[:, ts, :], ALU.add, ALU.subtract)
+            for ts in TILE_PAIRS:
+                nc.vector.scalar_tensor_tensor(share[:, ts, :], reach[:, ts, :], 0.0, least[:, ts, vs], ALU.max, ALU.min)
+            for ts in TILE_PAIRS:
+                nc.vector.scalar_tensor_tensor(cover[:, ts, :], both[:, ts, vs], 0.1 / 2, share[:, ts, :], ALU.add, ALU.subtract)
             nc.scalar.activation(root[:], cover[:], ACT.Abs_reciprocal_sqrt)
-            nc.scalar.activation(iv[:], root[:], ACT.Square)
-            share.append(sh)
-            inv.append(iv)
+            nc.scalar.activation(inverse[:], root[:], ACT.Square)
+            shares.append(share)
+            inverses.append(inverse)
 
-        accs = []
-        for h in range(2):
+        out_acc = []
+        for h in range(len(HALVES)):
             z_rows = tile("z_rows%d" % h, [P, PACK, HALF], BF16)
             for t in range(PACK):
-                nc.vector.scalar_tensor_tensor(z_rows[:, t, :], inv[h][:, t, :], gain[:, t : t + 1], share[h][:, t, :], ALU.mult, ALU.mult)
+                nc.vector.scalar_tensor_tensor(z_rows[:, t, :], inverses[h][:, t, :], gain[:, t : t + 1], shares[h][:, t, :], ALU.mult, ALU.mult)
             z_in = weave(nc.vector.tensor_copy, "z_in%d" % h, z_rows)
-            z_w = tile("z_w%d" % h, [P, HALF], U32)
-            z_s = tile("z_s%d" % h, [P, HALF], U8)
-            nc.vector.quantize_mx(out=z_w[:].bitcast(FP8X4), scales=z_s[:], in_=z_in[:])
-            for g, ts in enumerate(pairs):
-                acc = psum.tile([P, 2, HALF], F32, name="last%d%d" % (h, g), tag="bank%d" % (2 * h + g))
+            z_wd = tile("z_wd%d" % h, [P, HALF], U32)
+            z_sc = tile("z_sc%d" % h, [P, HALF], U8)
+            nc.vector.quantize_mx(out=z_wd[:].bitcast(FP8X4), scales=z_sc[:], in_=z_in[:])
+            for g, ts in enumerate(TILE_PAIRS):
+                acc = psum.tile([P, 2, HALF], F32, name="out_acc%d%d" % (h, g), tag="bank%d" % (2 * h + g))
                 for t in range(ts.start, ts.stop):
                     cols = slice(t * P, (t + 1) * P)
-                    nc.tensor.matmul_mx(out=acc[:, t - ts.start, :], lhsT=w3d[:, cols].bitcast(FP8X4), lhsT_scale=wsd[4:P, cols],
-                                        rhs=z_w[:].bitcast(FP8X4), rhs_scale=z_s[:], start=True, stop=True)
-                accs.append(acc)
-        copies = [nc.scalar.copy, nc.vector.tensor_copy]
-        o_in = []
-        for h, vs in enumerate(halves):
-            o_rows = tile("o_rows%d" % h, [P, PACK, HALF], F32)
-            for g, ts in enumerate(pairs):
-                nc.vector.tensor_tensor(o_rows[:, ts, :], accs[2 * h + g][:], resid[:, ts, vs], ALU.add)
-            nc.sync.dma_start(out_rows[:, :, vs], o_rows[:])
-            o_in.append(weave(copies[h], "o_in%d" % h, o_rows))
-        for h, vs in enumerate(halves):
-            o_w = tile("o_w%d" % h, [P, HALF], I32)
-            nc.vector.quantize_mx(out=o_w[:].bitcast(FP8X4), scales=o_s[:, vs], in_=o_in[h][:])
-            nc.sync.dma_start(out_words[:, vs], o_w[:])
-        for q in range(4):
+                    nc.tensor.matmul_mx(
+                        out=acc[:, t - ts.start, :], lhsT=w3_dealt[:, cols].bitcast(FP8X4), lhsT_scale=w3_sc_dealt[:, cols],
+                        rhs=z_wd[:].bitcast(FP8X4), rhs_scale=z_sc[:], start=True, stop=True,
+                    )
+                out_acc.append(acc)
+
+        rounders = [nc.scalar.copy, nc.vector.tensor_copy]
+        out_in = []
+        for h, vs in enumerate(HALVES):
+            result = tile("result%d" % h, [P, PACK, HALF], F32)
+            for g, ts in enumerate(TILE_PAIRS):
+                nc.vector.tensor_tensor(result[:, ts, :], out_acc[2 * h + g][:], resid[:, ts, vs], ALU.add)
+            nc.sync.dma_start(out_rows[:, :, vs], result[:])
+            out_in.append(weave(rounders[h], "out_in%d" % h, result))
+        for h, vs in enumerate(HALVES):
+            out_wd = tile("out_wd%d" % h, [P, HALF], I32)
+            nc.vector.quantize_mx(out=out_wd[:].bitcast(FP8X4), scales=out_sc[:, vs], in_=out_in[h][:])
+            nc.sync.dma_start(out_words[:, vs], out_wd[:])
+        for q in range(QUADRANTS):
             queue = nc.scalar if q % 2 else nc.sync
-            queue.dma_start(out_2[0, 4 * q : 4 * q + 4, :].bitcast(I32), o_s[32 * q : 32 * q + 4, :].bitcast(I32))
+            queue.dma_start(out_2[0, 4 * q : 4 * q + 4, :].bitcast(I32), out_sc[32 * q : 32 * q + 4, :].bitcast(I32))

from contextlib import ExitStack

import concourse.mybir as mybir

K, T, S, V, N, H = 512, 2048, 512, 256, 512, 512
FLOPS = 2 * K * H * S * 2 + 2 * H * N * V

F32 = mybir.dt.float32
BF16 = mybir.dt.bfloat16
I32 = mybir.dt.int32
U32 = mybir.dt.uint32
U16 = mybir.dt.uint16
U8 = mybir.dt.uint8
FP8X4 = mybir.dt.float8_e4m3fn_x4
ALU = mybir.AluOpType
ACT = mybir.ActivationFunctionType

P = 128
PACK = 4
QUADRANTS = 4
LINE = 16
HALF = V // 2
HALVES = [slice(0, HALF), slice(HALF, V)]
TILE_PAIRS = [slice(0, 2), slice(2, 4)]


def tile_picked_boxiou_none_po_kernel(
    tc, x_words, x_scales, w1_words, w1_scales, w2_words, w2_scales, gn, w3_words, w3_scales, res, offs, two, ba, bb, out_0, out_1, out_2
):
    nc = tc.nc
    with ExitStack() as ctx:
        keep = ctx.enter_context(tc.tile_pool(name="keep", bufs=1))
        psum = ctx.enter_context(tc.psum_pool(name="psum", bufs=1))

        def tile(name, shape, dtype, after=None):
            return keep.tile(shape, dtype, name=name, tag=after or name, align_bytes=64)

        def load_list(name, src):
            dst = tile(name, list(src.shape), U16)
            nc.sync.dma_start(dst[:], src)
            return dst

        def load_words(name, src, after=None):
            dst = tile(name, [P, src.shape[2]], I32, after)
            nc.sync.dma_start(dst[:], src[0].rearrange("p n t -> p (n t)").bitcast(I32))
            return dst

        def load_scales(queue, dst, src, quadrants=range(QUADRANTS)):
            for q in quadrants:
                queue.dma_start(dst[32 * q : 32 * q + 4, :].bitcast(I32), src[0, 4 * q : 4 * q + 4, :].bitcast(I32))

        def deal(name, src, dtype, run, after=None):
            dst = tile(name, [P, PACK * P], dtype, after)
            nc.gpsimd.tensor_copy(
                dst[:].rearrange("p (t c i) -> p c t i", t=PACK, i=run),
                src[:].rearrange("p (c i t) -> p c t i", t=PACK, i=run),
            )
            return dst

        def pick(name, window, dtype, offsets):
            dst = tile(name, [P, S], dtype)
            nc.vector.tensor_copy(dst[:], window.indirect(offsets[:]))
            return dst

        x_sc = tile("x_sc", [P, T], U8)
        nc.vector.memset(x_sc[:, : T // 2].bitcast(I32), 0)
        nc.gpsimd.memset(x_sc[:, T // 2 :].bitcast(I32), 0)
        w2_sc = tile("w2_sc", [P, H], U8)
        nc.gpsimd.memset(w2_sc[:].bitcast(I32), 0)
        w1_sc = tile("w1_sc", [P, H], U8)
        nc.gpsimd.memset(w1_sc[:].bitcast(I32), 0)

        load_scales(nc.gpsimd, w1_sc, w1_scales, range(QUADRANTS // 2, QUADRANTS))
        two_list = load_list("two_list", two)
        load_scales(nc.sync, x_sc, x_scales)
        idx_list = load_list("idx_list", offs)
        x_wd = load_words("x_wd", x_words)
        w2_wd = load_words("w2_wd", w2_words)
        load_scales(nc.sync, w2_sc, w2_scales)
        w1_wd = load_words("w1_wd", w1_words)
        load_scales(nc.sync, w1_sc, w1_scales, range(QUADRANTS // 2))
        ba_list = load_list("ba_list", ba)
        bb_list = load_list("bb_list", bb)

        two_sc = pick("two_sc", x_sc[:], U8, two_list)
        idx_sc = pick("idx_sc", x_sc[:], U8, idx_list)
        resid = tile("resid", [P, PACK, V], F32, "x_sc")
        nc.sync.dma_start(resid[:], res.rearrange("(p t) v -> p t v", t=PACK))
        two_wd = pick("two_wd", x_wd[:].bitcast(U32), U32, two_list)
        w2_dealt = deal("w2_dealt", w2_wd, I32, LINE // 4)
        w2_sc_dealt = deal("w2_sc_dealt", w2_sc, U8, LINE)
        w3_wd = load_words("w3_wd", w3_words, "w2_wd")

        def project(t, bank, words, scales, picked_words, picked_scales):
            acc = psum.tile([P, S], F32, name="acc%d" % bank, tag="bank%d" % bank)
            cols = slice(t * P, (t + 1) * P)
            nc.tensor.matmul_mx(
                out=acc[:], lhsT=words[:, cols].bitcast(FP8X4), lhsT_scale=scales[:, cols],
                rhs=picked_words[:].bitcast(FP8X4), rhs_scale=picked_scales[:], start=True, stop=True,
            )
            return acc

        def project_logits(t, bank):
            return project(t, bank, w2_dealt, w2_sc_dealt, two_wd, two_sc)

        def unload(name, acc):
            row = tile(name, [P, S], F32)
            nc.scalar.copy(row[:], acc[:])
            return row

        c_a = tile("c_a", [P, PACK, V], F32)
        c_b = tile("c_b", [P, PACK, V], F32)
        y_a = tile("y_a", [P, PACK, V], F32)
        y_diff = tile("y_diff", [P, PACK, V], F32)
        gap = tile("gap", [P, PACK, V], F32)

        def widths_on_scalar(t, logits):
            nc.scalar.activation(c_a[:, t, :], logits[:].indirect(ba_list[:]), ACT.Sigmoid)
            nc.scalar.activation(c_b[:, t, :], logits[:].indirect(bb_list[:]), ACT.Sigmoid)

        def middles_a(ts):
            for t in range(ts.start, ts.stop):
                nc.vector.tensor_copy(y_a[:, t, :], y_rows[t][:].indirect(ba_list[:]))

        def middles_b_minus_a(ts):
            for t in range(ts.start, ts.stop):
                nc.vector.tensor_tensor(y_diff[:, t, :], y_rows[t][:].indirect(bb_list[:]), y_a[:, t, :], ALU.subtract)

        def half_distance(ts):
            nc.scalar.activation(gap[:, ts, :], y_diff[:, ts, :], ACT.Abs, scale=0.5)

        logit_acc = [project_logits(t, t) for t in range(2)]
        idx_wd = pick("idx_wd", x_wd[:].bitcast(U32), U32, idx_list)
        w1_dealt = deal("w1_dealt", w1_wd, I32, LINE // 4)
        w1_sc_dealt = deal("w1_sc_dealt", w1_sc, U8, LINE, "w2_sc")
        y_acc = [project(t, PACK + t, w1_dealt, w1_sc_dealt, idx_wd, idx_sc) for t in range(PACK)]
        w3_dealt = deal("w3_dealt", w3_wd, I32, LINE // 4)
        w3_sc = tile("w3_sc", [P, N], U8, "idx_sc")
        nc.gpsimd.memset(w3_sc[:].bitcast(I32), 0)
        load_scales(nc.sync, w3_sc, w3_scales)
        w3_sc_dealt = deal("w3_sc_dealt", w3_sc, U8, LINE)
        both = tile("both", [P, PACK, V], F32, "w1_wd")
        least = tile("least", [P, PACK, V], F32, "w1_sc")

        low, high = TILE_PAIRS
        c_row = tile("c_row", [P, S], F32)
        nc.scalar.activation(c_row[:], logit_acc[0][:], ACT.Sigmoid)
        nc.vector.tensor_copy(c_a[:, 0, :], c_row[:].indirect(ba_list[:]))
        nc.vector.tensor_copy(c_b[:, 0, :], c_row[:].indirect(bb_list[:]))
        logits_1 = unload("logits_1", logit_acc[1])
        y_rows = [unload("y_row%d" % t, y_acc[t]) for t in range(low.start, low.stop)]
        middles_a(low)
        widths_on_scalar(1, logits_1)
        middles_b_minus_a(low)
        y_rows.extend(unload("y_row%d" % t, y_acc[t]) for t in range(high.start, high.stop))
        widths_on_scalar(2, unload("logits_2", project_logits(2, PACK + low.start)))
        middles_a(high)
        widths_on_scalar(3, unload("logits_3", project_logits(3, PACK + high.start)))
        half_distance(low)
        middles_b_minus_a(high)
        half_distance(high)
        for ts in TILE_PAIRS:
            nc.vector.tensor_tensor(both[:, ts, :], c_a[:, ts, :], c_b[:, ts, :], ALU.add)
            nc.vector.tensor_tensor(least[:, ts, :], c_a[:, ts, :], c_b[:, ts, :], ALU.min)

        gain = tile("gain", [P, PACK], F32, "two_sc")
        nc.sync.dma_start(gain[:], gn.rearrange("(p t) o -> p (t o)", t=PACK))
        out_rows = out_0.rearrange("(p t) v -> p t v", t=PACK)
        out_words = out_1[0].rearrange("p n t -> p (n t)").bitcast(I32)
        out_sc = tile("out_sc", [P, V], U8)

        def weave(copy, name, src):
            dst = tile(name, [P, HALF * PACK], BF16)
            copy(dst[:].rearrange("p (c i t) -> p c t i", i=4, t=PACK), src[:].rearrange("p t (c i) -> p c t i", i=4))
            return dst

        shares, inverses = [], []
        for h, vs in enumerate(HALVES):
            reach = tile("reach%d" % h, [P, PACK, HALF], F32)
            share = tile("share%d" % h, [P, PACK, HALF], F32)
            cover = tile("cover%d" % h, [P, PACK, HALF], F32)
            root = tile("root%d" % h, [P, PACK, HALF], F32)
            inverse = tile("inverse%d" % h, [P, PACK, HALF], F32)
            for ts in TILE_PAIRS:
                nc.vector.scalar_tensor_tensor(reach[:, ts, :], both[:, ts, vs], 0.5, gap[:, ts, vs], ALU.mult, ALU.subtract)
            for ts in TILE_PAIRS:
                nc.vector.scalar_tensor_tensor(share[:, ts, :], reach[:, ts, :], 0.0, least[:, ts, vs], ALU.max, ALU.min)
            for ts in TILE_PAIRS:
                nc.vector.scalar_tensor_tensor(cover[:, ts, :], both[:, ts, vs], 0.1 / 2, share[:, ts, :], ALU.add, ALU.subtract)
            nc.scalar.activation(root[:], cover[:], ACT.Abs_reciprocal_sqrt)
            nc.scalar.activation(inverse[:], root[:], ACT.Square)
            shares.append(share)
            inverses.append(inverse)

        out_acc = []
        for h in range(len(HALVES)):
            z_rows = tile("z_rows%d" % h, [P, PACK, HALF], BF16)
            for t in range(PACK):
                nc.vector.scalar_tensor_tensor(z_rows[:, t, :], inverses[h][:, t, :], gain[:, t : t + 1], shares[h][:, t, :], ALU.mult, ALU.mult)
            z_in = weave(nc.vector.tensor_copy, "z_in%d" % h, z_rows)
            z_wd = tile("z_wd%d" % h, [P, HALF], U32)
            z_sc = tile("z_sc%d" % h, [P, HALF], U8)
            nc.vector.quantize_mx(out=z_wd[:].bitcast(FP8X4), scales=z_sc[:], in_=z_in[:])
            for g, ts in enumerate(TILE_PAIRS):
                acc = psum.tile([P, 2, HALF], F32, name="out_acc%d%d" % (h, g), tag="bank%d" % (2 * h + g))
                for t in range(ts.start, ts.stop):
                    cols = slice(t * P, (t + 1) * P)
                    nc.tensor.matmul_mx(
                        out=acc[:, t - ts.start, :], lhsT=w3_dealt[:, cols].bitcast(FP8X4), lhsT_scale=w3_sc_dealt[:, cols],
                        rhs=z_wd[:].bitcast(FP8X4), rhs_scale=z_sc[:], start=True, stop=True,
                    )
                out_acc.append(acc)

        rounders = [nc.scalar.copy, nc.vector.tensor_copy]
        out_in = []
        for h, vs in enumerate(HALVES):
            result = tile("result%d" % h, [P, PACK, HALF], F32)
            for g, ts in enumerate(TILE_PAIRS):
                nc.vector.tensor_tensor(result[:, ts, :], out_acc[2 * h + g][:], resid[:, ts, vs], ALU.add)
            nc.sync.dma_start(out_rows[:, :, vs], result[:])
            out_in.append(weave(rounders[h], "out_in%d" % h, result))
        for h, vs in enumerate(HALVES):
            out_wd = tile("out_wd%d" % h, [P, HALF], I32)
            nc.vector.quantize_mx(out=out_wd[:].bitcast(FP8X4), scales=out_sc[:, vs], in_=out_in[h][:])
            nc.sync.dma_start(out_words[:, vs], out_wd[:])
        for q in range(QUADRANTS):
            queue = nc.scalar if q % 2 else nc.sync
            queue.dma_start(out_2[0, 4 * q : 4 * q + 4, :].bitcast(I32), out_sc[32 * q : 32 * q + 4, :].bitcast(I32))
